import numpy as np
import ml_dtypes


def mxq(x, axis, fmt="e4m3"):
    dtype, down = {"e4m3": (ml_dtypes.float8_e4m3fn, 7), "e5m2": (ml_dtypes.float8_e5m2, 14)}[fmt]
    v = np.moveaxis(np.asarray(x, np.float32).astype(ml_dtypes.bfloat16).astype(np.float64), axis, -1)
    blocks = v.reshape(v.shape[:-1] + (-1, 32))
    amax = np.abs(blocks).max(-1, keepdims=True)
    byte = np.maximum(np.where(amax > 0, np.frexp(amax)[1] - 1 + 127, 0) - down, 1)
    scale = np.exp2(byte - 127.0)
    codes = (blocks / scale).astype(np.float32).astype(dtype).astype(np.float64)
    return np.moveaxis((codes * scale).reshape(v.shape), -1, axis)


WIDE = False


def mx_kscale(k):
    if not WIDE:
        return np.ones(k)
    levels = np.array([10, -10, 5, -5, 0])
    if k % 512:
        return np.exp2(np.random.permutation(np.resize(levels, k // 32))).repeat(32)
    a = np.empty((k // 512, 16))
    for p in range(k // 512):
        a[p, :8] = np.random.permutation(np.resize(levels, 8))
        for g in range(8):
            far = levels[np.abs(levels - a[p, g]) >= 10]
            a[p, g + 8] = far[np.random.randint(len(far))]
    return np.exp2(a.ravel()).repeat(32)


def f64(x):
    return np.asarray(x).astype(np.float64)


def striped(idx):
    return np.tile(np.asarray(idx).reshape(-1, 16).T, (8, 1)).astype(np.uint16)


def unstriped(offs):
    return offs[:16].T.reshape(-1).astype(np.int64)


E2M1 = np.array([0.0, 0.5, 1.0, 1.5, 2.0, 3.0, 4.0, 6.0, -0.0, -0.5, -1.0, -1.5, -2.0, -3.0, -4.0, -6.0])


def pack_weight(w, fmt):
    k, n = w.shape
    w = f64(np.asarray(w, np.float32).astype(ml_dtypes.bfloat16)).reshape(k // 32, 32, n)
    amax = np.abs(w).max(1)
    if fmt == "e4m3":
        byte = np.frexp(amax)[1] - 1 + 127 - 7
    else:
        mant, ex = np.frexp(amax / 6.0)
        byte = np.where(mant > 0.5, ex, ex - 1) + 127
    byte = np.clip(np.where(amax > 0, byte, 1), 1, 254)
    scaled = (w * np.exp2(127.0 - byte)[:, None, :]).reshape(k, n).astype(np.float32)
    by_word = np.ascontiguousarray(scaled.reshape(k // 512, 128, 4, n).transpose(0, 1, 3, 2))
    if fmt == "e4m3":
        words = by_word.astype(ml_dtypes.float8_e4m3fn).view(np.uint8)
    else:
        c = by_word.astype(ml_dtypes.float4_e2m1fn).view(np.uint8) & 0xF
        words = (c[..., 0::2] | (c[..., 1::2] << 4)).reshape(k // 512, 128, 2 * n)
    return np.ascontiguousarray(words), np.ascontiguousarray(byte.astype(np.uint8).reshape(k // 512, 16, n))


def unpack_weight(words, scales, fmt):
    g, _, n = scales.shape
    words = np.ascontiguousarray(words).reshape(g, 128, n, -1)
    if fmt == "e4m3":
        vals = words.view(ml_dtypes.float8_e4m3fn).astype(np.float64)
    else:
        nib = np.empty((g, 128, n, 4), np.uint8)
        nib[..., 0::2] = words & 0xF
        nib[..., 1::2] = words >> 4
        vals = E2M1[nib]
    vals = vals * np.repeat(np.exp2(scales.astype(np.float64) - 127.0), 8, axis=1)[..., None]
    return vals.transpose(0, 1, 3, 2).reshape(g * 512, n)


def softplus(v):
    return np.log(1.0 + np.exp(v))


D, K, R, T, I, Q, G = 512, 512, 512, 2048, 512, 128, 64


def setup_inputs():
    n = np.random.standard_normal
    idx = np.random.permutation(T)[:I]
    fd = mx_kscale(D)
    fk = mx_kscale(K)
    fi = mx_kscale(I)
    keysp = pack_weight(n((D, T)) / fd[:, None], "e2m1")
    tabp = pack_weight(n((K, T)) / fk[:, None], "e2m1")
    return {
        "query": (n((D, Q)) * 0.9 / np.sqrt(D) * fd[:, None]).astype(np.float32),
        "keys_words": keysp[0],
        "keys_scales": keysp[1],
        "th": (np.random.uniform(-0.3, 0.6, (Q, 1))).astype(np.float32),
        "reserve": (np.random.uniform(50.0, 200.0, (Q, 1))).astype(np.float32),
        "tab_words": tabp[0],
        "tab_scales": tabp[1],
        "w1": (n((K, R)) * 1 / np.sqrt(K) * fk[:, None]).astype(np.float32),
        "temper": (np.random.uniform(0.4, 1.0, (R, 1))).astype(np.float32),
        "os": (np.random.uniform(4.0, 16.0, (1, I)) * fi).astype(np.float32),
        "vs": (np.random.uniform(0.5, 2.0, (1, I)) / fi).astype(np.float32),
        "offs": striped(idx),
    }


def reference(query, keys_words, keys_scales, th, reserve, tab_words, tab_scales, w1, temper, os, vs, offs):
    idx = unstriped(offs)
    keysu = unpack_weight(keys_words, keys_scales, "e2m1")
    tabu = unpack_weight(tab_words, tab_scales, "e2m1")
    queryq = mxq(f64(query), 0, "e4m3")
    keysidxg = keysu[:, idx]
    a = queryq.T @ keysidxg
    p = softplus(a - f64(th))
    z = np.sum(p, axis=1, keepdims=True) + f64(reserve)
    w = p / z
    w1q = mxq(f64(w1), 0, "e4m3")
    tabidxg = tabu[:, idx]
    zh = w1q.T @ tabidxg
    ht = np.exp(zh * f64(temper))
    mz = ht.reshape(R, G, I // G).sum(axis=2)
    mzr = np.repeat(mz, I // G, axis=1)
    hv = ht / mzr * 4.0
    wo1 = w * f64(os)
    wt1 = wo1.T
    hw = hv * f64(vs)
    ht1 = hw.T
    wt1q = mxq(wt1, 0, "e4m3")
    ht1q = mxq(ht1, 0, "e4m3")
    o = wt1q.T @ ht1q
    return o

@@ -1,0 +1,228 @@
+from contextlib import ExitStack
+
+import concourse.mybir as mybir
+from concourse.masks import make_identity
+
+D, K, R, T, I, Q = 512, 512, 512, 2048, 512, 128
+P = 128
+FLOPS = 2 * (D * Q * I + K * R * I + I * Q * R)
+
+F32 = mybir.dt.float32
+BF16 = mybir.dt.bfloat16
+I32 = mybir.dt.int32
+U32 = mybir.dt.uint32
+U16 = mybir.dt.uint16
+U8 = mybir.dt.uint8
+FP8X4 = mybir.dt.float8_e4m3fn_x4
+FP4X4 = mybir.dt.float4_e2m1fn_x4
+ACT = mybir.ActivationFunctionType
+ALU = mybir.AluOpType
+
+
+def tile_attend_lrshared_capped_kernel(tc, query, keys_words, keys_scales, th, reserve, tab_words,
+                                        tab_scales, w1, temper, slot_factor, vs, offs, out):
+    nc = tc.nc
+    with ExitStack() as ctx:
+        sb = ctx.enter_context(tc.tile_pool(name="sb", bufs=1))
+        shared = ctx.enter_context(tc.tile_pool(name="shared", bufs=1))
+        ps = ctx.enter_context(tc.psum_pool(name="ps", bufs=1))
+
+        def tile(name, cols, dtype):
+            return sb.tile([P, cols], dtype, name=name, align_bytes=64)
+
+        def bank(name, n):
+            return ps.tile([P, 512], F32, name=name, tag="bank%d" % n)
+
+        def load_scales(queue, window, scales):
+            for quad in range(4):
+                queue.dma_start(out=window[32 * quad : 32 * quad + 4, :].bitcast(I32),
+                                    in_=scales[0, 4 * quad : 4 * quad + 4, :].bitcast(I32))
+
+        def placed(name, shape, dtype, offset):
+            return shared.tile(shape, dtype, name=name, offset=offset, align_bytes=64)
+
+        offsets = sb.tile([P, I // 16], U16, name="offsets")
+        nc.sync.dma_start(offsets[:], offs)
+        vs_c = placed("vs_c", [P, 3136], F32, 0)
+        nc.sync.dma_start(out=vs_c[:, 0:4], in_=vs.rearrange("o (p t) -> p (o t)", t=4))
+
+        ident = tile("ident", P, F32)
+        tab_w = tile("tab_w", T, U16)
+        tab_s = placed("tab_s", [P, T], U8, 12544)
+        make_identity(nc, ident[:])
+        nc.vector.memset(tab_s[:].bitcast(I32), 0)
+        nc.sync.dma_start(out=tab_w[:].bitcast(I32), in_=tab_words[0].bitcast(I32))
+        load_scales(nc.sync, tab_s, tab_scales)
+
+        def load_w(a, dst):
+            nc.sync.dma_start(out=dst[:], in_=w1[:, 256 * a : 256 * (a + 1)].rearrange("(p t) r -> p t r", t=4))
+            return dst
+
+        w_raw = [load_w(0, sb.tile([P, 4, 256], F32, name="w_raw0", align_bytes=64))]
+
+        vs4 = tile("vs4", 4, F32)
+        nc.scalar.activation(out=vs4[:], in_=vs_c[:, 0:4], func=ACT.Copy, scale=4.0)
+        vs_p = bank("vs_p", 1)
+        for t in range(4):
+            nc.tensor.transpose(vs_p[:, P * t : P * (t + 1)], vs4[:, t : t + 1].to_broadcast([P, P]), ident[:])
+        vs_b = tile("vs_b", I, F32)
+        nc.scalar.copy(out=vs_b[:].rearrange("p (h w g e) -> p h w g e", h=2, w=2, e=2),
+                       in_=vs_p[:].rearrange("p (w e g h) -> p h w g e", h=2, w=2, e=2))
+
+        key_s = placed("key_s", [P, T], U8, 0)
+        key_w = placed("key_w", [P, T], U16, 2048)
+        q_raw = placed("q_raw", [P, 4, Q], F32, 6144)
+        temper_c = placed("temper_c", [P, 4], F32, 12288)
+        th_c = placed("th_c", [P, 1], F32, 12352)
+        os_c = placed("os_c", [P, 4], F32, 12416)
+        res_c = placed("res_c", [P, 1], F32, 12480)
+        nc.gpsimd.memset(key_s[:].bitcast(I32), 0)
+        w_raw.append(load_w(1, placed("w_raw1", [P, 4, 256], F32, 8192)))
+        with nc.allow_non_contiguous_dma(reason="one temper to a partition and tile"):
+            nc.sync.dma_start(out=temper_c[:], in_=temper.rearrange("(j p) o -> p (j o)", p=P))
+        nc.sync.dma_start(out=q_raw[:], in_=query.rearrange("(p t) q -> p t q", t=4))
+        nc.sync.dma_start(out=key_w[:].bitcast(I32), in_=keys_words[0].bitcast(I32))
+        load_scales(nc.sync, key_s, keys_scales)
+        nc.sync.dma_start(out=th_c[:], in_=th)
+        nc.sync.dma_start(out=os_c[:], in_=slot_factor.rearrange("o (p t) -> p (o t)", t=4))
+        nc.sync.dma_start(out=res_c[:], in_=reserve)
+
+        tab_gw = tile("tab_gw", I, U16)
+        tab_gs = tile("tab_gs", I, U8)
+        nc.vector.tensor_copy(tab_gw[:], tab_w[:].indirect(offsets[:]))
+        nc.vector.tensor_copy(tab_gs[:], tab_s[:].indirect(offsets[:]))
+
+        def cast_interleaved(dst, src):
+            nc.scalar.activation(out=dst.rearrange("p (c i t) -> p c t i", i=4, t=4),
+                                 in_=src.rearrange("p t (c i) -> p c t i", i=4), func=ACT.Copy)
+
+        def quantise(name, src, cols, codes):
+            scales = tile(name + "_s", cols, U8)
+            nc.vector.quantize_mx(out=codes[:].bitcast(FP8X4), scales=scales[:], in_=src)
+            return codes, scales
+
+        w_q = []
+        for j in range(4):
+            w_bf = tile("w_bf%d" % j, 512, BF16)
+            cast_interleaved(w_bf[:], w_raw[j // 2][:, :, 128 * (j % 2) : 128 * (j % 2 + 1)])
+            w_q.append(quantise("w_q%d" % j, w_bf[:], P, placed("w_c%d" % j, [P, P], U32, 12544 + 512 * j)))
+
+        ht = [tile("ht%d" % a, 2 * I, F32) for a in range(2)]
+        for j in range(4):
+            zh = bank("zh%d" % j, 1 + j)
+            nc.tensor.matmul_mx(out=zh[:], lhsT=w_q[j][0][:].bitcast(FP8X4), lhsT_scale=w_q[j][1][:],
+                                rhs=tab_gw[:].bitcast(FP4X4), rhs_scale=tab_gs[:], start=True, stop=True)
+            nc.scalar.activation(
+                out=ht[j // 2][:].rearrange("p (c j g e) -> p j c g e", c=4, j=2, e=2)[:, j % 2],
+                in_=zh[:].rearrange("p (g c e) -> p c g e", c=4, e=2),
+                func=ACT.Exp, scale=temper_c[:, j : j + 1])
+
+        key_gw = tile("key_gw", I, U16)
+        key_gs = tile("key_gs", I, U8)
+        nc.vector.tensor_copy(key_gw[:], key_w[:].indirect(offsets[:]))
+        nc.vector.tensor_copy(key_gs[:], key_s[:].indirect(offsets[:]))
+        q_bf = tile("q_bf", 512, BF16)
+        nc.gpsimd.tensor_scalar(out=q_bf[:].rearrange("p (q t) -> p q t", t=4),
+                                in0=q_raw[:].rearrange("p t q -> p q t"),
+                                scalar1=1.0, scalar2=0.0, op0=ALU.mult, op1=ALU.add)
+        q_c, q_s = quantise("q_q", q_bf[:], P, tile("q_c", P, U32))
+        neg_th = tile("neg_th", 1, F32)
+        nc.gpsimd.tensor_scalar(out=neg_th[:], in0=th_c[:], scalar1=-1.0, scalar2=0.0, op0=ALU.mult, op1=ALU.add)
+
+        hs = []
+        rc_p = []
+        for a in range(2):
+            sr = bank("sr%d" % a, 5 + a)
+            terms = ht[a][:].rearrange("p (c m e) -> p c e m", c=4, e=2)
+            for u in range(8):
+                nc.tensor.matmul(out=sr[:, 0:P], lhsT=terms[:, u // 2, u % 2, :], rhs=ident[:],
+                                 start=(u == 0), stop=(u == 7), is_transpose=True)
+            if a == 0:
+                sc = bank("sc", 0)
+                nc.tensor.matmul_mx(out=sc[:], lhsT=q_c[:].bitcast(FP8X4), lhsT_scale=q_s[:],
+                                    rhs=key_gw[:].bitcast(FP4X4), rhs_scale=key_gs[:], start=True, stop=True)
+            for jj in range(2):
+                s_ = tile("hs%d" % (2 * a + jj), I, F32)
+                nc.gpsimd.tensor_tensor(
+                    out=s_[:].rearrange("p (c m) -> p c m", c=4),
+                    in0=ht[a][:].rearrange("p (c j m) -> p j c m", c=4, j=2)[:, jj],
+                    in1=vs_b[:].rearrange("p (c m) -> p c m", c=4), op=ALU.mult)
+                hs.append(s_)
+            rc_t = placed("rc_t%d" % a, [P, P], F32, 512 * a)
+            nc.vector.reciprocal(out=rc_t[:], in_=sr[:, 0:P])
+            nc.tensor.transpose(sr[:, P : 2 * P], rc_t[:], ident[:])
+            rc_p.append(sr)
+
+        sc_v = sc[:].rearrange("p (m w e) -> p w m e", w=2, e=2)
+        mag = tile("mag", I, F32)
+        pos = tile("pos", I, F32)
+        tail_wide = placed("tail", [P, 2 * I], F32, 14592)
+        tail = tail_wide[:, 0:I]
+        lg = tile("lg", I, F32)
+        sp = tile("sp", I, F32)
+        pos_sum = tile("pos_sum", 1, F32)
+        lg_sum = placed("lg_sum", [P, 1], F32, 12288)
+        nc.scalar.activation(out=mag[:].rearrange("p (w m e) -> p w m e", w=2, e=2), in_=sc_v, func=ACT.Abs,
+                             bias=neg_th[:])
+        nc.scalar.activation(out=tail, in_=mag[:], func=ACT.Exp, scale=-1.0)
+        nc.scalar.activation(out=pos[:].rearrange("p (w m e) -> p w m e", w=2, e=2), in_=sc_v, func=ACT.Relu,
+                             bias=neg_th[:], accum_out=pos_sum[:])
+        nc.scalar.activation(out=lg[:], in_=tail, func=ACT.Ln, bias=1.0, accum_out=lg_sum[:])
+        os_p = bank("os_p", 7)
+        for t in range(4):
+            nc.tensor.transpose(os_p[:, P * t : P * (t + 1)], os_c[:, t : t + 1].to_broadcast([P, P]), ident[:])
+
+        def turn(name, n, src, dst):
+            tp = bank(name + "_p", n)
+            words = src[:].bitcast(F32)
+            for w in range(2):
+                nc.tensor.transpose(tp[:, P * w : P * (w + 1)], words[:, P * w : P * (w + 1)], ident[:])
+            nc.scalar.copy(out=dst[:].bitcast(F32).rearrange("p (r w) -> p r w", w=2),
+                           in_=tp[:, 0 : 2 * P].rearrange("p (w r) -> p r w", w=2))
+            return dst
+
+        h_codes = [tile("h_c%d" % a, 2 * P, U32) for a in range(2)]
+        h_scales = [tile("h_s%d" % a, 2 * P, U8) for a in range(2)]
+        h_t = []
+        for j in range(4):
+            hw = tile("hw%d" % j, I, BF16)
+            lo = P + 64 * (j % 2)
+            rc = rc_p[j // 2][:, lo : lo + 64].unsqueeze(2).unsqueeze(3).broadcast_to([P, 64, 2, 2])
+            for w in range(2):
+                nc.vector.tensor_tensor(
+                    out=hw[:].rearrange("p (w g h e) -> p w g h e", w=2, h=2, e=2)[:, w],
+                    in0=hs[j][:].rearrange("p (h w g e) -> p w g h e", w=2, h=2, e=2)[:, w],
+                    in1=rc, op=ALU.mult)
+            h_t.append(turn("h_t%d" % j, 1 + j, hw, placed("h_t%d" % j, [P, 512], BF16, 14592 + 1024 * j)))
+
+        z = tile("z", 1, F32)
+        nc.vector.scalar_tensor_tensor(out=z[:], in0=pos_sum[:], scalar=lg_sum[:], in1=res_c[:],
+                                       op0=ALU.add, op1=ALU.add)
+        rz = tile("rz", 1, F32)
+        nc.vector.reciprocal(out=rz[:], in_=z[:])
+        nc.vector.tensor_tensor(out=sp[:], in0=lg[:], in1=pos[:], op=ALU.add)
+        wo = tile("wo", I, BF16)
+        for w in range(2):
+            nc.vector.scalar_tensor_tensor(
+                out=wo[:, 256 * w : 256 * (w + 1)].rearrange("p (m e) -> p m e", e=2),
+                in0=sp[:, 256 * w : 256 * (w + 1)].rearrange("p (m e) -> p m e", e=2),
+                scalar=rz[:],
+                in1=os_p[:, 256 * w : 256 * (w + 1)].rearrange("p (e m) -> p m e", e=2),
+                op0=ALU.mult, op1=ALU.mult)
+        w_t = turn("w_t", 0, wo, tile("w_t", 512, BF16))
+        wt_c, wt_s = quantise("wt_q", w_t[:], P, tile("wt_c", P, U32))
+
+        for a in range(2):
+            for jj in range(2):
+                cols = slice(P * jj, P * (jj + 1))
+                nc.vector.quantize_mx(out=h_codes[a][:, cols].bitcast(FP8X4), scales=h_scales[a][:, cols],
+                                      in_=h_t[2 * a + jj][:])
+            o_p = bank("o_p%d" % a, 5 + a)
+            nc.tensor.matmul_mx(out=o_p[:, 0:256], lhsT=wt_c[:].bitcast(FP8X4), lhsT_scale=wt_s[:],
+                                rhs=h_codes[a][:].bitcast(FP8X4), rhs_scale=h_scales[a][:], start=True, stop=True)
+            o_s = tile("o_s%d" % a, 256, F32)
+            if a == 0:
+                nc.scalar.copy(out=o_s[:], in_=o_p[:, 0:256])
+            else:
+                nc.vector.tensor_copy(out=o_s[:], in_=o_p[:, 0:256])
+            nc.sync.dma_start(out=out[:, 256 * a : 256 * (a + 1)], in_=o_s[:])

@@ -43,12 +43,12 @@ def tile_attend_lrshared_capped_kernel(tc, query, keys_words, keys_scales, th, r
 
         offsets = sb.tile([P, I // 16], U16, name="offsets")
         nc.sync.dma_start(offsets[:], offs)
-        vs_c = placed("vs_c", [P, 3136], F32, 0)
+        vs_c = placed("vs_c", [P, 3168], F32, 0)
         nc.sync.dma_start(out=vs_c[:, 0:4], in_=vs.rearrange("o (p t) -> p (o t)", t=4))
 
         ident = tile("ident", P, F32)
         tab_w = tile("tab_w", T, U16)
-        tab_s = placed("tab_s", [P, T], U8, 12544)
+        tab_s = placed("tab_s", [P, T], U8, 12672)
         make_identity(nc, ident[:])
         nc.vector.memset(tab_s[:].bitcast(I32), 0)
         nc.sync.dma_start(out=tab_w[:].bitcast(I32), in_=tab_words[0].bitcast(I32))
@@ -60,28 +60,30 @@ def tile_attend_lrshared_capped_kernel(tc, query, keys_words, keys_scales, th, r
 
         w_raw = [load_w(0, sb.tile([P, 4, 256], F32, name="w_raw0", align_bytes=64))]
 
-        vs4 = tile("vs4", 4, F32)
-        nc.scalar.activation(out=vs4[:], in_=vs_c[:, 0:4], func=ACT.Copy, scale=4.0)
+        vs4 = placed("vs4", [P, 1024], F32, 18816)
+        nc.vector.tensor_scalar(out=vs4[:, 0:4], in0=vs_c[:, 0:4], scalar1=4.0, scalar2=None, op0=ALU.mult)
         vs_p = bank("vs_p", 1)
         for t in range(4):
             nc.tensor.transpose(vs_p[:, P * t : P * (t + 1)], vs4[:, t : t + 1].to_broadcast([P, P]), ident[:])
         vs_b = tile("vs_b", I, F32)
-        nc.scalar.copy(out=vs_b[:].rearrange("p (h w g e) -> p h w g e", h=2, w=2, e=2),
-                       in_=vs_p[:].rearrange("p (w e g h) -> p h w g e", h=2, w=2, e=2))
+        for h in range(2):
+            nc.scalar.activation(out=vs_b[:].rearrange("p (h w g e) -> p h w g e", h=2, w=2, e=2)[:, h],
+                                 in_=vs_p[:].rearrange("p (w e g h) -> p h w g e", h=2, w=2, e=2)[:, h],
+                                 func=ACT.Copy)
 
         key_s = placed("key_s", [P, T], U8, 0)
         key_w = placed("key_w", [P, T], U16, 2048)
         q_raw = placed("q_raw", [P, 4, Q], F32, 6144)
-        temper_c = placed("temper_c", [P, 4], F32, 12288)
-        th_c = placed("th_c", [P, 1], F32, 12352)
-        os_c = placed("os_c", [P, 4], F32, 12416)
-        res_c = placed("res_c", [P, 1], F32, 12480)
-        nc.gpsimd.memset(key_s[:].bitcast(I32), 0)
+        temper_c = placed("temper_c", [P, 32], F32, 12288)
+        th_c = placed("th_c", [P, 1], F32, 12416)
+        os_c = placed("os_c", [P, 4], F32, 12480)
+        res_c = placed("res_c", [P, 1], F32, 12544)
+        nc.vector.memset(key_s[:].bitcast(I32), 0)
         w_raw.append(load_w(1, placed("w_raw1", [P, 4, 256], F32, 8192)))
         with nc.allow_non_contiguous_dma(reason="one temper to a partition and tile"):
-            nc.sync.dma_start(out=temper_c[:], in_=temper.rearrange("(j p) o -> p (j o)", p=P))
-        nc.sync.dma_start(out=q_raw[:], in_=query.rearrange("(p t) q -> p t q", t=4))
+            nc.sync.dma_start(out=temper_c[:, 0:4], in_=temper.rearrange("(j p) o -> p (j o)", p=P))
         nc.sync.dma_start(out=key_w[:].bitcast(I32), in_=keys_words[0].bitcast(I32))
+        nc.sync.dma_start(out=q_raw[:], in_=query.rearrange("(p t) q -> p t q", t=4))
         load_scales(nc.sync, key_s, keys_scales)
         nc.sync.dma_start(out=th_c[:], in_=th)
         nc.sync.dma_start(out=os_c[:], in_=slot_factor.rearrange("o (p t) -> p (o t)", t=4))
@@ -103,9 +105,9 @@ def tile_attend_lrshared_capped_kernel(tc, query, keys_words, keys_scales, th, r
 
         w_q = []
         for j in range(4):
-            w_bf = tile("w_bf%d" % j, 512, BF16)
+            w_bf = placed("w_bf%d" % j, [P, 512], BF16, 18816 + 1024 * j)
             cast_interleaved(w_bf[:], w_raw[j // 2][:, :, 128 * (j % 2) : 128 * (j % 2 + 1)])
-            w_q.append(quantise("w_q%d" % j, w_bf[:], P, placed("w_c%d" % j, [P, P], U32, 12544 + 512 * j)))
+            w_q.append(quantise("w_q%d" % j, w_bf[:], P, placed("w_c%d" % j, [P, P], U32, 12672 + 512 * j)))
 
         ht = [tile("ht%d" % a, 2 * I, F32) for a in range(2)]
         for j in range(4):
@@ -117,17 +119,17 @@ def tile_attend_lrshared_capped_kernel(tc, query, keys_words, keys_scales, th, r
                 in_=zh[:].rearrange("p (g c e) -> p c g e", c=4, e=2),
                 func=ACT.Exp, scale=temper_c[:, j : j + 1])
 
-        key_gw = tile("key_gw", I, U16)
-        key_gs = tile("key_gs", I, U8)
+        key_gw = placed("key_gw", [P, I], U16, 18816 + 2560)
+        key_gs = placed("key_gs", [P, I], U8, 18816 + 3584)
         nc.vector.tensor_copy(key_gw[:], key_w[:].indirect(offsets[:]))
         nc.vector.tensor_copy(key_gs[:], key_s[:].indirect(offsets[:]))
         q_bf = tile("q_bf", 512, BF16)
         nc.gpsimd.tensor_scalar(out=q_bf[:].rearrange("p (q t) -> p q t", t=4),
                                 in0=q_raw[:].rearrange("p t q -> p q t"),
                                 scalar1=1.0, scalar2=0.0, op0=ALU.mult, op1=ALU.add)
-        q_c, q_s = quantise("q_q", q_bf[:], P, tile("q_c", P, U32))
-        neg_th = tile("neg_th", 1, F32)
-        nc.gpsimd.tensor_scalar(out=neg_th[:], in0=th_c[:], scalar1=-1.0, scalar2=0.0, op0=ALU.mult, op1=ALU.add)
+        q_c, q_s = quantise("q_q", q_bf[:], P, placed("q_c", [P, P], U32, 2048))
+        neg_th = placed("neg_th", [P, 1], F32, 12352)
+        nc.scalar.activation(out=neg_th[:], in_=th_c[:], func=ACT.Copy, scale=-1.0)
 
         hs = []
         rc_p = []
@@ -138,7 +140,7 @@ def tile_attend_lrshared_capped_kernel(tc, query, keys_words, keys_scales, th, r
                 nc.tensor.matmul(out=sr[:, 0:P], lhsT=terms[:, u // 2, u % 2, :], rhs=ident[:],
                                  start=(u == 0), stop=(u == 7), is_transpose=True)
             if a == 0:
-                sc = bank("sc", 0)
+                sc = bank("sc", 2)
                 nc.tensor.matmul_mx(out=sc[:], lhsT=q_c[:].bitcast(FP8X4), lhsT_scale=q_s[:],
                                     rhs=key_gw[:].bitcast(FP4X4), rhs_scale=key_gs[:], start=True, stop=True)
             for jj in range(2):
@@ -156,7 +158,7 @@ def tile_attend_lrshared_capped_kernel(tc, query, keys_words, keys_scales, th, r
         sc_v = sc[:].rearrange("p (m w e) -> p w m e", w=2, e=2)
         mag = tile("mag", I, F32)
         pos = tile("pos", I, F32)
-        tail_wide = placed("tail", [P, 2 * I], F32, 14592)
+        tail_wide = placed("tail", [P, 2 * I], F32, 14720)
         tail = tail_wide[:, 0:I]
         lg = tile("lg", I, F32)
         sp = tile("sp", I, F32)
@@ -193,7 +195,7 @@ def tile_attend_lrshared_capped_kernel(tc, query, keys_words, keys_scales, th, r
                     out=hw[:].rearrange("p (w g h e) -> p w g h e", w=2, h=2, e=2)[:, w],
                     in0=hs[j][:].rearrange("p (h w g e) -> p w g h e", w=2, h=2, e=2)[:, w],
                     in1=rc, op=ALU.mult)
-            h_t.append(turn("h_t%d" % j, 1 + j, hw, placed("h_t%d" % j, [P, 512], BF16, 14592 + 1024 * j)))
+            h_t.append(turn("h_t%d" % j, 1 + j, hw, placed("h_t%d" % j, [P, 512], BF16, 14720 + 1024 * j)))
 
         z = tile("z", 1, F32)
         nc.vector.scalar_tensor_tensor(out=z[:], in0=pos_sum[:], scalar=lg_sum[:], in1=res_c[:],
@@ -222,7 +224,7 @@ def tile_attend_lrshared_capped_kernel(tc, query, keys_words, keys_scales, th, r
                                 rhs=h_codes[a][:].bitcast(FP8X4), rhs_scale=h_scales[a][:], start=True, stop=True)
             o_s = tile("o_s%d" % a, 256, F32)
             if a == 0:
-                nc.scalar.copy(out=o_s[:], in_=o_p[:, 0:256])
-            else:
                 nc.vector.tensor_copy(out=o_s[:], in_=o_p[:, 0:256])
+            else:
+                nc.scalar.copy(out=o_s[:], in_=o_p[:, 0:256])
             nc.sync.dma_start(out=out[:, 256 * a : 256 * (a + 1)], in_=o_s[:])

from contextlib import ExitStack

import concourse.mybir as mybir
from concourse.masks import make_identity

D, K, R, T, I, Q = 512, 512, 512, 2048, 512, 128
P = 128
FLOPS = 2 * (D * Q * I + K * R * I + I * Q * R)

F32 = mybir.dt.float32
BF16 = mybir.dt.bfloat16
I32 = mybir.dt.int32
U32 = mybir.dt.uint32
U16 = mybir.dt.uint16
U8 = mybir.dt.uint8
FP8X4 = mybir.dt.float8_e4m3fn_x4
FP4X4 = mybir.dt.float4_e2m1fn_x4
ACT = mybir.ActivationFunctionType
ALU = mybir.AluOpType


def tile_attend_lrshared_capped_kernel(tc, query, keys_words, keys_scales, th, reserve, tab_words,
                                        tab_scales, w1, temper, slot_factor, vs, offs, out):
    nc = tc.nc
    with ExitStack() as ctx:
        sb = ctx.enter_context(tc.tile_pool(name="sb", bufs=1))
        shared = ctx.enter_context(tc.tile_pool(name="shared", bufs=1))
        ps = ctx.enter_context(tc.psum_pool(name="ps", bufs=1))

        def tile(name, cols, dtype):
            return sb.tile([P, cols], dtype, name=name, align_bytes=64)

        def bank(name, n):
            return ps.tile([P, 512], F32, name=name, tag="bank%d" % n)

        def load_scales(queue, window, scales):
            for quad in range(4):
                queue.dma_start(out=window[32 * quad : 32 * quad + 4, :].bitcast(I32),
                                    in_=scales[0, 4 * quad : 4 * quad + 4, :].bitcast(I32))

        def placed(name, shape, dtype, offset):
            return shared.tile(shape, dtype, name=name, offset=offset, align_bytes=64)

        offsets = sb.tile([P, I // 16], U16, name="offsets")
        nc.sync.dma_start(offsets[:], offs)
        vs_c = placed("vs_c", [P, 3168], F32, 0)
        nc.sync.dma_start(out=vs_c[:, 0:4], in_=vs.rearrange("o (p t) -> p (o t)", t=4))

        ident = tile("ident", P, F32)
        tab_w = tile("tab_w", T, U16)
        tab_s = placed("tab_s", [P, T], U8, 12672)
        make_identity(nc, ident[:])
        nc.vector.memset(tab_s[:].bitcast(I32), 0)
        nc.sync.dma_start(out=tab_w[:].bitcast(I32), in_=tab_words[0].bitcast(I32))
        load_scales(nc.sync, tab_s, tab_scales)

        def load_w(a, dst):
            nc.sync.dma_start(out=dst[:], in_=w1[:, 256 * a : 256 * (a + 1)].rearrange("(p t) r -> p t r", t=4))
            return dst

        w_raw = [load_w(0, sb.tile([P, 4, 256], F32, name="w_raw0", align_bytes=64))]

        vs4 = placed("vs4", [P, 1024], F32, 18816)
        nc.vector.tensor_scalar(out=vs4[:, 0:4], in0=vs_c[:, 0:4], scalar1=4.0, scalar2=None, op0=ALU.mult)
        vs_p = bank("vs_p", 1)
        for t in range(4):
            nc.tensor.transpose(vs_p[:, P * t : P * (t + 1)], vs4[:, t : t + 1].to_broadcast([P, P]), ident[:])
        vs_b = tile("vs_b", I, F32)
        for h in range(2):
            nc.scalar.activation(out=vs_b[:].rearrange("p (h w g e) -> p h w g e", h=2, w=2, e=2)[:, h],
                                 in_=vs_p[:].rearrange("p (w e g h) -> p h w g e", h=2, w=2, e=2)[:, h],
                                 func=ACT.Copy)

        key_s = placed("key_s", [P, T], U8, 0)
        key_w = placed("key_w", [P, T], U16, 2048)
        q_raw = placed("q_raw", [P, 4, Q], F32, 6144)
        temper_c = placed("temper_c", [P, 32], F32, 12288)
        th_c = placed("th_c", [P, 1], F32, 12416)
        os_c = placed("os_c", [P, 4], F32, 12480)
        res_c = placed("res_c", [P, 1], F32, 12544)
        nc.vector.memset(key_s[:].bitcast(I32), 0)
        w_raw.append(load_w(1, placed("w_raw1", [P, 4, 256], F32, 8192)))
        with nc.allow_non_contiguous_dma(reason="one temper to a partition and tile"):
            nc.sync.dma_start(out=temper_c[:, 0:4], in_=temper.rearrange("(j p) o -> p (j o)", p=P))
        nc.sync.dma_start(out=key_w[:].bitcast(I32), in_=keys_words[0].bitcast(I32))
        nc.sync.dma_start(out=q_raw[:], in_=query.rearrange("(p t) q -> p t q", t=4))
        load_scales(nc.sync, key_s, keys_scales)
        nc.sync.dma_start(out=th_c[:], in_=th)
        nc.sync.dma_start(out=os_c[:], in_=slot_factor.rearrange("o (p t) -> p (o t)", t=4))
        nc.sync.dma_start(out=res_c[:], in_=reserve)

        tab_gw = tile("tab_gw", I, U16)
        tab_gs = tile("tab_gs", I, U8)
        nc.vector.tensor_copy(tab_gw[:], tab_w[:].indirect(offsets[:]))
        nc.vector.tensor_copy(tab_gs[:], tab_s[:].indirect(offsets[:]))

        def cast_interleaved(dst, src):
            nc.scalar.activation(out=dst.rearrange("p (c i t) -> p c t i", i=4, t=4),
                                 in_=src.rearrange("p t (c i) -> p c t i", i=4), func=ACT.Copy)

        def quantise(name, src, cols, codes):
            scales = tile(name + "_s", cols, U8)
            nc.vector.quantize_mx(out=codes[:].bitcast(FP8X4), scales=scales[:], in_=src)
            return codes, scales

        w_q = []
        for j in range(4):
            w_bf = placed("w_bf%d" % j, [P, 512], BF16, 18816 + 1024 * j)
            cast_interleaved(w_bf[:], w_raw[j // 2][:, :, 128 * (j % 2) : 128 * (j % 2 + 1)])
            w_q.append(quantise("w_q%d" % j, w_bf[:], P, placed("w_c%d" % j, [P, P], U32, 12672 + 512 * j)))

        ht = [tile("ht%d" % a, 2 * I, F32) for a in range(2)]
        for j in range(4):
            zh = bank("zh%d" % j, 1 + j)
            nc.tensor.matmul_mx(out=zh[:], lhsT=w_q[j][0][:].bitcast(FP8X4), lhsT_scale=w_q[j][1][:],
                                rhs=tab_gw[:].bitcast(FP4X4), rhs_scale=tab_gs[:], start=True, stop=True)
            nc.scalar.activation(
                out=ht[j // 2][:].rearrange("p (c j g e) -> p j c g e", c=4, j=2, e=2)[:, j % 2],
                in_=zh[:].rearrange("p (g c e) -> p c g e", c=4, e=2),
                func=ACT.Exp, scale=temper_c[:, j : j + 1])

        key_gw = placed("key_gw", [P, I], U16, 18816 + 2560)
        key_gs = placed("key_gs", [P, I], U8, 18816 + 3584)
        nc.vector.tensor_copy(key_gw[:], key_w[:].indirect(offsets[:]))
        nc.vector.tensor_copy(key_gs[:], key_s[:].indirect(offsets[:]))
        q_bf = tile("q_bf", 512, BF16)
        nc.gpsimd.tensor_scalar(out=q_bf[:].rearrange("p (q t) -> p q t", t=4),
                                in0=q_raw[:].rearrange("p t q -> p q t"),
                                scalar1=1.0, scalar2=0.0, op0=ALU.mult, op1=ALU.add)
        q_c, q_s = quantise("q_q", q_bf[:], P, placed("q_c", [P, P], U32, 2048))
        neg_th = placed("neg_th", [P, 1], F32, 12352)
        nc.scalar.activation(out=neg_th[:], in_=th_c[:], func=ACT.Copy, scale=-1.0)

        hs = []
        rc_p = []
        for a in range(2):
            sr = bank("sr%d" % a, 5 + a)
            terms = ht[a][:].rearrange("p (c m e) -> p c e m", c=4, e=2)
            for u in range(8):
                nc.tensor.matmul(out=sr[:, 0:P], lhsT=terms[:, u // 2, u % 2, :], rhs=ident[:],
                                 start=(u == 0), stop=(u == 7), is_transpose=True)
            if a == 0:
                sc = bank("sc", 2)
                nc.tensor.matmul_mx(out=sc[:], lhsT=q_c[:].bitcast(FP8X4), lhsT_scale=q_s[:],
                                    rhs=key_gw[:].bitcast(FP4X4), rhs_scale=key_gs[:], start=True, stop=True)
            for jj in range(2):
                s_ = tile("hs%d" % (2 * a + jj), I, F32)
                nc.gpsimd.tensor_tensor(
                    out=s_[:].rearrange("p (c m) -> p c m", c=4),
                    in0=ht[a][:].rearrange("p (c j m) -> p j c m", c=4, j=2)[:, jj],
                    in1=vs_b[:].rearrange("p (c m) -> p c m", c=4), op=ALU.mult)
                hs.append(s_)
            rc_t = placed("rc_t%d" % a, [P, P], F32, 512 * a)
            nc.vector.reciprocal(out=rc_t[:], in_=sr[:, 0:P])
            nc.tensor.transpose(sr[:, P : 2 * P], rc_t[:], ident[:])
            rc_p.append(sr)

        sc_v = sc[:].rearrange("p (m w e) -> p w m e", w=2, e=2)
        mag = tile("mag", I, F32)
        pos = tile("pos", I, F32)
        tail_wide = placed("tail", [P, 2 * I], F32, 14720)
        tail = tail_wide[:, 0:I]
        lg = tile("lg", I, F32)
        sp = tile("sp", I, F32)
        pos_sum = tile("pos_sum", 1, F32)
        lg_sum = placed("lg_sum", [P, 1], F32, 12288)
        nc.scalar.activation(out=mag[:].rearrange("p (w m e) -> p w m e", w=2, e=2), in_=sc_v, func=ACT.Abs,
                             bias=neg_th[:])
        nc.scalar.activation(out=tail, in_=mag[:], func=ACT.Exp, scale=-1.0)
        nc.scalar.activation(out=pos[:].rearrange("p (w m e) -> p w m e", w=2, e=2), in_=sc_v, func=ACT.Relu,
                             bias=neg_th[:], accum_out=pos_sum[:])
        nc.scalar.activation(out=lg[:], in_=tail, func=ACT.Ln, bias=1.0, accum_out=lg_sum[:])
        os_p = bank("os_p", 7)
        for t in range(4):
            nc.tensor.transpose(os_p[:, P * t : P * (t + 1)], os_c[:, t : t + 1].to_broadcast([P, P]), ident[:])

        def turn(name, n, src, dst):
            tp = bank(name + "_p", n)
            words = src[:].bitcast(F32)
            for w in range(2):
                nc.tensor.transpose(tp[:, P * w : P * (w + 1)], words[:, P * w : P * (w + 1)], ident[:])
            nc.scalar.copy(out=dst[:].bitcast(F32).rearrange("p (r w) -> p r w", w=2),
                           in_=tp[:, 0 : 2 * P].rearrange("p (w r) -> p r w", w=2))
            return dst

        h_codes = [tile("h_c%d" % a, 2 * P, U32) for a in range(2)]
        h_scales = [tile("h_s%d" % a, 2 * P, U8) for a in range(2)]
        h_t = []
        for j in range(4):
            hw = tile("hw%d" % j, I, BF16)
            lo = P + 64 * (j % 2)
            rc = rc_p[j // 2][:, lo : lo + 64].unsqueeze(2).unsqueeze(3).broadcast_to([P, 64, 2, 2])
            for w in range(2):
                nc.vector.tensor_tensor(
                    out=hw[:].rearrange("p (w g h e) -> p w g h e", w=2, h=2, e=2)[:, w],
                    in0=hs[j][:].rearrange("p (h w g e) -> p w g h e", w=2, h=2, e=2)[:, w],
                    in1=rc, op=ALU.mult)
            h_t.append(turn("h_t%d" % j, 1 + j, hw, placed("h_t%d" % j, [P, 512], BF16, 14720 + 1024 * j)))

        z = tile("z", 1, F32)
        nc.vector.scalar_tensor_tensor(out=z[:], in0=pos_sum[:], scalar=lg_sum[:], in1=res_c[:],
                                       op0=ALU.add, op1=ALU.add)
        rz = tile("rz", 1, F32)
        nc.vector.reciprocal(out=rz[:], in_=z[:])
        nc.vector.tensor_tensor(out=sp[:], in0=lg[:], in1=pos[:], op=ALU.add)
        wo = tile("wo", I, BF16)
        for w in range(2):
            nc.vector.scalar_tensor_tensor(
                out=wo[:, 256 * w : 256 * (w + 1)].rearrange("p (m e) -> p m e", e=2),
                in0=sp[:, 256 * w : 256 * (w + 1)].rearrange("p (m e) -> p m e", e=2),
                scalar=rz[:],
                in1=os_p[:, 256 * w : 256 * (w + 1)].rearrange("p (e m) -> p m e", e=2),
                op0=ALU.mult, op1=ALU.mult)
        w_t = turn("w_t", 0, wo, tile("w_t", 512, BF16))
        wt_c, wt_s = quantise("wt_q", w_t[:], P, tile("wt_c", P, U32))

        for a in range(2):
            for jj in range(2):
                cols = slice(P * jj, P * (jj + 1))
                nc.vector.quantize_mx(out=h_codes[a][:, cols].bitcast(FP8X4), scales=h_scales[a][:, cols],
                                      in_=h_t[2 * a + jj][:])
            o_p = bank("o_p%d" % a, 5 + a)
            nc.tensor.matmul_mx(out=o_p[:, 0:256], lhsT=wt_c[:].bitcast(FP8X4), lhsT_scale=wt_s[:],
                                rhs=h_codes[a][:].bitcast(FP8X4), rhs_scale=h_scales[a][:], start=True, stop=True)
            o_s = tile("o_s%d" % a, 256, F32)
            if a == 0:
                nc.vector.tensor_copy(out=o_s[:], in_=o_p[:, 0:256])
            else:
                nc.scalar.copy(out=o_s[:], in_=o_p[:, 0:256])
            nc.sync.dma_start(out=out[:, 256 * a : 256 * (a + 1)], in_=o_s[:])
